import numpy as np
import ml_dtypes


def mxq(x, axis, fmt="e4m3"):
    dtype, down = {"e4m3": (ml_dtypes.float8_e4m3fn, 7), "e5m2": (ml_dtypes.float8_e5m2, 14)}[fmt]
    v = np.moveaxis(np.asarray(x, np.float32).astype(ml_dtypes.bfloat16).astype(np.float64), axis, -1)
    blocks = v.reshape(v.shape[:-1] + (-1, 32))
    amax = np.abs(blocks).max(-1, keepdims=True)
    byte = np.maximum(np.where(amax > 0, np.frexp(amax)[1] - 1 + 127, 0) - down, 1)
    scale = np.exp2(byte - 127.0)
    codes = (blocks / scale).astype(np.float32).astype(dtype).astype(np.float64)
    return np.moveaxis((codes * scale).reshape(v.shape), -1, axis)


WIDE = False


def mx_kscale(k):
    if not WIDE:
        return np.ones(k)
    levels = np.array([10, -10, 5, -5, 0])
    if k % 512:
        return np.exp2(np.random.permutation(np.resize(levels, k // 32))).repeat(32)
    a = np.empty((k // 512, 16))
    for p in range(k // 512):
        a[p, :8] = np.random.permutation(np.resize(levels, 8))
        for g in range(8):
            far = levels[np.abs(levels - a[p, g]) >= 10]
            a[p, g + 8] = far[np.random.randint(len(far))]
    return np.exp2(a.ravel()).repeat(32)


def f64(x):
    return np.asarray(x).astype(np.float64)


def striped(idx):
    return np.tile(np.asarray(idx).reshape(-1, 16).T, (8, 1)).astype(np.uint16)


def unstriped(offs):
    return offs[:16].T.reshape(-1).astype(np.int64)


E2M1 = np.array([0.0, 0.5, 1.0, 1.5, 2.0, 3.0, 4.0, 6.0, -0.0, -0.5, -1.0, -1.5, -2.0, -3.0, -4.0, -6.0])


def pack_weight(w, fmt):
    k, n = w.shape
    w = f64(np.asarray(w, np.float32).astype(ml_dtypes.bfloat16)).reshape(k // 32, 32, n)
    amax = np.abs(w).max(1)
    if fmt == "e4m3":
        byte = np.frexp(amax)[1] - 1 + 127 - 7
    else:
        mant, ex = np.frexp(amax / 6.0)
        byte = np.where(mant > 0.5, ex, ex - 1) + 127
    byte = np.clip(np.where(amax > 0, byte, 1), 1, 254)
    scaled = (w * np.exp2(127.0 - byte)[:, None, :]).reshape(k, n).astype(np.float32)
    by_word = np.ascontiguousarray(scaled.reshape(k // 512, 128, 4, n).transpose(0, 1, 3, 2))
    if fmt == "e4m3":
        words = by_word.astype(ml_dtypes.float8_e4m3fn).view(np.uint8)
    else:
        c = by_word.astype(ml_dtypes.float4_e2m1fn).view(np.uint8) & 0xF
        words = (c[..., 0::2] | (c[..., 1::2] << 4)).reshape(k // 512, 128, 2 * n)
    return np.ascontiguousarray(words), np.ascontiguousarray(byte.astype(np.uint8).reshape(k // 512, 16, n))


def unpack_weight(words, scales, fmt):
    g, _, n = scales.shape
    words = np.ascontiguousarray(words).reshape(g, 128, n, -1)
    if fmt == "e4m3":
        vals = words.view(ml_dtypes.float8_e4m3fn).astype(np.float64)
    else:
        nib = np.empty((g, 128, n, 4), np.uint8)
        nib[..., 0::2] = words & 0xF
        nib[..., 1::2] = words >> 4
        vals = E2M1[nib]
    vals = vals * np.repeat(np.exp2(scales.astype(np.float64) - 127.0), 8, axis=1)[..., None]
    return vals.transpose(0, 1, 3, 2).reshape(g * 512, n)


D, E, T, I, Q = 512, 512, 2048, 512, 128


def setup_inputs():
    n = np.random.standard_normal
    idx2 = np.random.permutation(I)[:I]
    idx = np.random.permutation(T)[:I]
    fd = mx_kscale(D)
    fe = mx_kscale(E)
    keysp = pack_weight(n((D, T)) / fd[:, None], "e2m1")
    valsp = pack_weight(n((E, T)) / fe[:, None], "e2m1")
    return {
        "query": (n((D, Q)) * 0.7 / np.sqrt(D) * fd[:, None]).astype(np.float32),
        "keys_words": keysp[0],
        "keys_scales": keysp[1],
        "gout": (n((E, Q)) * 1 / np.sqrt(E) * fe[:, None]).astype(np.float32),
        "vals_words": valsp[0],
        "vals_scales": valsp[1],
        "base": (0.5 * n((Q, I))).astype(np.float32),
        "offs2": striped(idx2),
        "offs": striped(idx),
    }


def reference(query, keys_words, keys_scales, gout, vals_words, vals_scales, base, offs2, offs):
    idx2 = unstriped(offs2)
    idx = unstriped(offs)
    keysu = unpack_weight(keys_words, keys_scales, "e2m1")
    valsu = unpack_weight(vals_words, vals_scales, "e2m1")
    queryq = mxq(f64(query), 0, "e4m3")
    keysidxg = keysu[:, idx]
    a = queryq.T @ keysidxg
    pa = np.exp(a)
    pb = np.sqrt(pa)
    p = pa * pb[:, idx2]
    z = np.sum(p, axis=1, keepdims=True)
    goutq = mxq(f64(gout), 0, "e4m3")
    valsidxg = valsu[:, idx]
    c0 = goutq.T @ valsidxg
    dz = np.sum(c0 * p / np.square(z) * (-1.0), axis=1, keepdims=True)
    dp = c0 / z + dz
    e1 = dp * pa
    s1 = np.zeros((Q, I))
    s1[:, idx2] = e1
    dpa = dp * pb[:, idx2] + s1 * 0.5 / np.sqrt(pa)
    da = dpa * pa
    hda = da * 512.0 * 2.0 * 512.0
    hdpa = hda * pa
    hs1 = hdpa / np.sqrt(pa) * 0.5
    he1 = hs1[:, idx2]
    hdp = hdpa * pb[:, idx2] + he1 * pa
    hdz = np.sum(hdp, axis=1, keepdims=True)
    hz = np.sum(hdp * c0 / np.square(z) * (-1.0), axis=1, keepdims=True) + np.sum(hdz * (-1.0) * c0 * p / np.square(np.square(z)) * (-1.0), axis=1, keepdims=True) * z * 2.0
    hp = hdz * (-1.0) / np.square(z) * c0 + hz
    e51 = hdpa * dp
    s51 = np.zeros((Q, I))
    s51[:, idx2] = e51
    e52 = hp * pa
    s52 = np.zeros((Q, I))
    s52[:, idx2] = e52
    hpb = s51 + s52
    hpa = hda * dpa + hdpa * s1 * 0.5 / np.square(np.sqrt(pa)) * (-1.0) * 0.5 / np.sqrt(pa) + he1 * dp + hp * pb[:, idx2] + hpb * 0.5 / np.sqrt(pa)
    ha = hpa * pa
    y = ha + f64(base)
    return y

@@ -1,0 +1,178 @@
+from contextlib import ExitStack
+
+import concourse.mybir as mybir
+from concourse.masks import make_identity
+
+F32 = mybir.dt.float32
+BF16 = mybir.dt.bfloat16
+I32 = mybir.dt.int32
+U32 = mybir.dt.uint32
+U16 = mybir.dt.uint16
+U8 = mybir.dt.uint8
+FP8X4 = mybir.dt.float8_e4m3fn_x4
+FP4X4 = mybir.dt.float4_e2m1fn_x4
+ALU = mybir.AluOpType
+ACT = mybir.ActivationFunctionType
+
+P = 128
+PACK = 4
+D, T, I, Q = 512, 2048, 512, 128
+GAIN = 512.0 * 2.0 * 512.0
+GATHER_COLS = 544
+SCATTER_COPY_COLS = 704
+SCATTER_ADD_COLS = 1024
+FLOPS = 2 * 2 * D * Q * I
+
+
+def tile_attend_gplinkedproduct_kernel(tc, query, keys_words, keys_scales, gout, vals_words, vals_scales, base, offs2, offs, out):
+    nc = tc.nc
+    with ExitStack() as ctx:
+        sb = ctx.enter_context(tc.tile_pool(name="sb", bufs=1))
+        shared = ctx.enter_context(tc.tile_pool(name="shared", bufs=1))
+        ps = ctx.enter_context(tc.psum_pool(name="ps", bufs=1))
+
+        def wide(name, cols=I):
+            return sb.tile([P, cols], F32, name=name, align_bytes=64)
+
+        def column(name):
+            return sb.tile([P, 1], F32, name=name)
+
+        tokens = sb.tile([P, I // 16], U16, name="tokens")
+        links = sb.tile([P, I // 16], U16, name="links")
+        k_words = sb.tile([P, T], U16, name="k_words", align_bytes=64)
+        v_words = sb.tile([P, T], U16, name="v_words", align_bytes=64)
+        k_scales = sb.tile([P, T], U8, name="k_scales", align_bytes=64)
+        v_scales = sb.tile([P, T], U8, name="v_scales", align_bytes=64)
+        q_raw = sb.tile([P, PACK, Q], F32, name="q_raw")
+        g_raw = sb.tile([P, PACK, Q], F32, name="g_raw")
+        base_sb = wide("base_sb")
+
+        def load_scales(queue, tile, rows):
+            for quad in range(4):
+                queue.dma_start(out=tile[32 * quad : 32 * quad + 4, :].bitcast(I32), in_=rows[0, 4 * quad : 4 * quad + 4, :].bitcast(I32))
+
+        nc.gpsimd.memset(k_scales[:].bitcast(I32), 0)
+        nc.sync.dma_start(tokens[:], offs)
+        nc.sync.dma_start(out=k_words[:].bitcast(I32), in_=keys_words[0].bitcast(I32))
+        load_scales(nc.scalar, k_scales, keys_scales)
+        nc.vector.memset(v_scales[:].bitcast(I32), 0)
+        nc.sync.dma_start(out=q_raw[:], in_=query.rearrange("(p j) w -> p j w", j=PACK))
+        nc.sync.dma_start(out=v_words[:].bitcast(I32), in_=vals_words[0].bitcast(I32))
+        nc.sync.dma_start(out=g_raw[:], in_=gout.rearrange("(p j) w -> p j w", j=PACK))
+        load_scales(nc.sync, v_scales, vals_scales)
+        nc.sync.dma_start(links[:], offs2)
+        nc.sync.dma_start(out=base_sb[:], in_=base)
+
+        pb = wide("pb", GATHER_COLS)
+        hs1 = wide("hs1", GATHER_COLS)
+        nc.gpsimd.memset(pb[:, I:], 0.0)
+        nc.gpsimd.memset(hs1[:, I:], 0.0)
+        warm = column("warm")
+        nc.scalar.activation(warm[:], hs1[:, I : I + 1], ACT.Exp)
+        ident = sb.tile([P, P], F32, name="ident")
+        make_identity(nc, ident[:])
+
+        def interleave(name, raw, offset):
+            grouped = shared.tile([P, Q, PACK], BF16, name=name, align_bytes=64, offset=offset)
+            nc.scalar.copy(grouped[:], raw[:].rearrange("p j w -> p w j"))
+            return grouped
+
+        def quantize(name, grouped):
+            codes = sb.tile([P, Q], U32, name=name + "_codes", align_bytes=64)
+            scales = sb.tile([P, Q], U8, name=name + "_scales", align_bytes=64)
+            nc.vector.quantize_mx(out=codes[:].bitcast(FP8X4), scales=scales[:], in_=grouped[:].rearrange("p w j -> p (w j)"))
+            return codes, scales
+
+        def gather(name, table, dtype, offset):
+            picked = shared.tile([P, I], dtype, name=name, align_bytes=64, offset=offset)
+            nc.vector.tensor_copy(picked[:], table[:].indirect(tokens[:]))
+            return picked
+
+        def product(name, codes, scales, words, word_scales):
+            acc = ps.tile([P, I], F32, name=name)
+            nc.tensor.matmul_mx(out=acc[:], lhsT=codes[:].bitcast(FP8X4), lhsT_scale=scales[:], rhs=words[:].bitcast(FP4X4), rhs_scale=word_scales[:], start=True, stop=True)
+            return acc
+
+        q_grouped = interleave("q_grouped", q_raw, 0)
+        ks = gather("ks", k_scales, U8, 4096)
+        kw = gather("kw", k_words, U16, 5120)
+        q_codes, q_scales = quantize("q", q_grouped)
+        a = product("a", q_codes, q_scales, kw, ks)
+        g_grouped = interleave("g_grouped", g_raw, 2048)
+        vw = gather("vw", v_words, U16, 512)
+        vs = gather("vs", v_scales, U8, 0)
+        g_codes, g_scales = quantize("g", g_grouped)
+        c0 = product("c0", g_codes, g_scales, vw, vs)
+
+        pa = wide("pa")
+        nc.scalar.activation(pb[:, :I], a[:], ACT.Exp, scale=0.5)
+        nc.scalar.activation(pa[:], a[:], ACT.Exp)
+        p = shared.tile([P, I], F32, name="p", align_bytes=64, offset=2048)
+        nc.vector.tensor_tensor(p[:], pb[:].indirect(links[:]), pa[:], ALU.mult)
+        z = column("z")
+        spare_a = wide("spare_a")
+        nc.scalar.activation(spare_a[:], p[:], ACT.Copy, accum_out=z[:])
+        cp_sum = column("cp_sum")
+        spare_v = wide("spare_v")
+        nc.vector.scalar_tensor_tensor(spare_v[:], c0[:], 1.0, p[:], ALU.mult, ALU.mult, accum_out=cp_sum[:])
+        rz = column("rz")
+        nc.vector.reciprocal(rz[:], z[:])
+        mean = column("mean")
+        nc.vector.tensor_scalar(mean[:], cp_sum[:], rz[:], None, ALU.mult)
+        u = wide("u")
+        nc.vector.scalar_tensor_tensor(u[:], c0[:], mean[:], p[:], ALU.subtract, ALU.mult)
+        su = wide("su", SCATTER_COPY_COLS)
+        nc.vector.tensor_copy(su[:].indirect(links[:]), u[:])
+
+        w = wide("w")
+        pa_z = wide("pa_z")
+        nc.scalar.activation(w[:], p[:], ACT.Copy, scale=rz[:])
+        nc.scalar.activation(pa_z[:], pa[:], ACT.Copy, scale=rz[:])
+        half_gain = column("half_gain")
+        gain = column("gain")
+        neg_rz = column("neg_rz")
+        nc.scalar.activation(half_gain[:], rz[:], ACT.Copy, scale=0.5 * GAIN)
+        nc.scalar.activation(gain[:], rz[:], ACT.Copy, scale=GAIN)
+        nc.scalar.activation(neg_rz[:], rz[:], ACT.Copy, scale=-1.0)
+        neg_gain_w = wide("neg_gain_w")
+        nc.scalar.activation(neg_gain_w[:], w[:], ACT.Copy, scale=-GAIN)
+
+        da = wide("da")
+        nc.vector.scalar_tensor_tensor(da[:], su[:, :I], 0.5, u[:], ALU.mult, ALU.add)
+        nc.vector.scalar_tensor_tensor(hs1[:, :I], da[:], half_gain[:], pb[:, :I], ALU.mult, ALU.mult)
+        direct = wide("direct")
+        nc.vector.scalar_tensor_tensor(direct[:], da[:], gain[:], w[:], ALU.mult, ALU.mult)
+        linked = wide("linked")
+        nc.vector.tensor_tensor(linked[:], hs1[:].indirect(links[:]), pa_z[:], ALU.mult)
+
+        da_sq = column("da_sq")
+        nc.scalar.activation(spare_a[:], da[:], ACT.Square, scale=rz[:], accum_out=da_sq[:])
+        y2 = wide("y2")
+        nc.scalar.activation(y2[:], neg_gain_w[:], ACT.Copy, scale=da_sq[:])
+        neg_da = wide("neg_da")
+        nc.scalar.activation(neg_da[:], da[:], ACT.Copy, scale=neg_rz[:])
+
+        hdp = wide("hdp")
+        hdz = column("hdz")
+        nc.vector.scalar_tensor_tensor(hdp[:], linked[:], 1.0, direct[:], ALU.mult, ALU.add, accum_out=hdz[:])
+        r1 = wide("r1")
+        nc.vector.scalar_tensor_tensor(r1[:], c0[:], mean[:], hdp[:], ALU.subtract, ALU.mult)
+        sr = wide("sr", SCATTER_ADD_COLS)
+        nc.vector.tensor_tensor(sr[:].indirect(links[:]), r1[:], y2[:], ALU.add)
+        y3 = wide("y3")
+        nc.scalar.activation(y3[:], neg_da[:], ACT.Copy, scale=hdz[:])
+
+        terms = (y2, base_sb, r1, y3)
+        turned = [ps.tile([P, P], F32, name="turned%d" % b) for b in range(I // P)]
+        for n, term in enumerate(terms):
+            for b in range(I // P):
+                nc.tensor.matmul(turned[b][:], term[:, b * P : (b + 1) * P], ident[:], start=(n == 0), stop=(n == len(terms) - 1), is_transpose=True)
+        rest = ps.tile([P, I], F32, name="rest")
+        for b in range(I // P):
+            turned_sb = sb.tile([P, P], F32, name="turned_sb%d" % b)
+            nc.scalar.copy(turned_sb[:], turned[b][:])
+            nc.tensor.transpose(rest[:, b * P : (b + 1) * P], turned_sb[:], ident[:])
+
+        result = wide("result")
+        nc.vector.scalar_tensor_tensor(result[:], sr[:, :I], 0.5, rest[:], ALU.mult, ALU.add)
+        nc.sync.dma_start(out=out, in_=result[:])

@@ -18,7 +18,9 @@ P = 128
 PACK = 4
 D, T, I, Q = 512, 2048, 512, 128
 GAIN = 512.0 * 2.0 * 512.0
-GATHER_COLS = 544
+HALF = I // 2
+HALVES = (slice(0, HALF), slice(HALF, I))
+LINK_HALVES = (slice(0, HALF // 16), slice(HALF // 16, I // 16))
 SCATTER_COPY_COLS = 704
 SCATTER_ADD_COLS = 1024
 FLOPS = 2 * 2 * D * Q * I
@@ -41,34 +43,32 @@ def tile_attend_gplinkedproduct_kernel(tc, query, keys_words, keys_scales, gout,
         links = sb.tile([P, I // 16], U16, name="links")
         k_words = sb.tile([P, T], U16, name="k_words", align_bytes=64)
         v_words = sb.tile([P, T], U16, name="v_words", align_bytes=64)
-        k_scales = sb.tile([P, T], U8, name="k_scales", align_bytes=64)
+        k_scales = shared.tile([P, T], U8, name="k_scales", align_bytes=64, offset=8192)
         v_scales = sb.tile([P, T], U8, name="v_scales", align_bytes=64)
-        q_raw = sb.tile([P, PACK, Q], F32, name="q_raw")
-        g_raw = sb.tile([P, PACK, Q], F32, name="g_raw")
-        base_sb = wide("base_sb")
+        q_raw = shared.tile([P, PACK, Q], F32, name="q_raw", offset=6144)
+        g_raw = shared.tile([P, PACK, Q], F32, name="g_raw", offset=2048)
 
         def load_scales(queue, tile, rows):
             for quad in range(4):
                 queue.dma_start(out=tile[32 * quad : 32 * quad + 4, :].bitcast(I32), in_=rows[0, 4 * quad : 4 * quad + 4, :].bitcast(I32))
 
+        pb = wide("pb")
+        hs1 = wide("hs1")
+        zero = column("zero")
         nc.gpsimd.memset(k_scales[:].bitcast(I32), 0)
+        nc.gpsimd.memset(zero[:], 0.0)
+        nc.vector.memset(v_scales[:].bitcast(I32), 0)
         nc.sync.dma_start(tokens[:], offs)
         nc.sync.dma_start(out=k_words[:].bitcast(I32), in_=keys_words[0].bitcast(I32))
         load_scales(nc.scalar, k_scales, keys_scales)
-        nc.vector.memset(v_scales[:].bitcast(I32), 0)
         nc.sync.dma_start(out=q_raw[:], in_=query.rearrange("(p j) w -> p j w", j=PACK))
-        nc.sync.dma_start(out=v_words[:].bitcast(I32), in_=vals_words[0].bitcast(I32))
-        nc.sync.dma_start(out=g_raw[:], in_=gout.rearrange("(p j) w -> p j w", j=PACK))
+        nc.gpsimd.dma_start(out=v_words[:].bitcast(I32), in_=vals_words[0].bitcast(I32))
+        nc.gpsimd.dma_start(out=g_raw[:], in_=gout.rearrange("(p j) w -> p j w", j=PACK))
         load_scales(nc.sync, v_scales, vals_scales)
         nc.sync.dma_start(links[:], offs2)
-        nc.sync.dma_start(out=base_sb[:], in_=base)
 
-        pb = wide("pb", GATHER_COLS)
-        hs1 = wide("hs1", GATHER_COLS)
-        nc.gpsimd.memset(pb[:, I:], 0.0)
-        nc.gpsimd.memset(hs1[:, I:], 0.0)
         warm = column("warm")
-        nc.scalar.activation(warm[:], hs1[:, I : I + 1], ACT.Exp)
+        nc.scalar.activation(warm[:], zero[:], ACT.Exp)
         ident = sb.tile([P, P], F32, name="ident")
         make_identity(nc, ident[:])
 
@@ -93,32 +93,38 @@ def tile_attend_gplinkedproduct_kernel(tc, query, keys_words, keys_scales, gout,
             nc.tensor.matmul_mx(out=acc[:], lhsT=codes[:].bitcast(FP8X4), lhsT_scale=scales[:], rhs=words[:].bitcast(FP4X4), rhs_scale=word_scales[:], start=True, stop=True)
             return acc
 
-        q_grouped = interleave("q_grouped", q_raw, 0)
+        q_grouped = interleave("q_grouped", q_raw, 10240)
         ks = gather("ks", k_scales, U8, 4096)
         kw = gather("kw", k_words, U16, 5120)
         q_codes, q_scales = quantize("q", q_grouped)
         a = product("a", q_codes, q_scales, kw, ks)
-        g_grouped = interleave("g_grouped", g_raw, 2048)
-        vw = gather("vw", v_words, U16, 512)
+        g_grouped = interleave("g_grouped", g_raw, 6144)
+        base_sb = shared.tile([P, I], F32, name="base_sb", offset=2048)
+        nc.sync.dma_start(out=base_sb[:], in_=base)
+        vw = gather("vw", v_words, U16, 9728)
         vs = gather("vs", v_scales, U8, 0)
         g_codes, g_scales = quantize("g", g_grouped)
         c0 = product("c0", g_codes, g_scales, vw, vs)
 
         pa = wide("pa")
-        nc.scalar.activation(pb[:, :I], a[:], ACT.Exp, scale=0.5)
+        nc.scalar.activation(pb[:], a[:], ACT.Exp, scale=0.5)
         nc.scalar.activation(pa[:], a[:], ACT.Exp)
-        p = shared.tile([P, I], F32, name="p", align_bytes=64, offset=2048)
-        nc.vector.tensor_tensor(p[:], pb[:].indirect(links[:]), pa[:], ALU.mult)
+        p = shared.tile([P, I], F32, name="p", align_bytes=64, offset=6144)
+        for cols, entries in zip(HALVES, LINK_HALVES):
+            nc.vector.tensor_tensor(p[:, cols], pb[:].indirect(links[:, entries]), pa[:, cols], ALU.mult)
+        z_first = column("z_first")
         z = column("z")
         spare_a = wide("spare_a")
-        nc.scalar.activation(spare_a[:], p[:], ACT.Copy, accum_out=z[:])
-        cp_sum = column("cp_sum")
+        nc.scalar.activation(spare_a[:, HALVES[0]], p[:, HALVES[0]], ACT.Copy, scale=1.0 / HALF, accum_out=z_first[:])
+        nc.scalar.activation(spare_a[:, HALVES[1]], p[:, HALVES[1]], ACT.Identity, bias=z_first[:], accum_out=z[:])
+        cp_sums = [column("cp_sum%d" % h) for h in range(2)]
         spare_v = wide("spare_v")
-        nc.vector.scalar_tensor_tensor(spare_v[:], c0[:], 1.0, p[:], ALU.mult, ALU.mult, accum_out=cp_sum[:])
+        for cols, cp_sum in zip(HALVES, cp_sums):
+            nc.vector.scalar_tensor_tensor(spare_v[:, cols], c0[:, cols], 1.0, p[:, cols], ALU.mult, ALU.mult, accum_out=cp_sum[:])
         rz = column("rz")
         nc.vector.reciprocal(rz[:], z[:])
         mean = column("mean")
-        nc.vector.tensor_scalar(mean[:], cp_sum[:], rz[:], None, ALU.mult)
+        nc.vector.tensor_scalar(mean[:], cp_sums[0][:], cp_sums[1][:], rz[:], ALU.add, ALU.mult)
         u = wide("u")
         nc.vector.scalar_tensor_tensor(u[:], c0[:], mean[:], p[:], ALU.subtract, ALU.mult)
         su = wide("su", SCATTER_COPY_COLS)
@@ -138,12 +144,15 @@ def tile_attend_gplinkedproduct_kernel(tc, query, keys_words, keys_scales, gout,
         nc.scalar.activation(neg_gain_w[:], w[:], ACT.Copy, scale=-GAIN)
 
         da = wide("da")
-        nc.vector.scalar_tensor_tensor(da[:], su[:, :I], 0.5, u[:], ALU.mult, ALU.add)
-        nc.vector.scalar_tensor_tensor(hs1[:, :I], da[:], half_gain[:], pb[:, :I], ALU.mult, ALU.mult)
+        for cols in HALVES:
+            nc.vector.scalar_tensor_tensor(da[:, cols], su[:, cols], 0.5, u[:, cols], ALU.mult, ALU.add)
+        for cols in HALVES:
+            nc.vector.scalar_tensor_tensor(hs1[:, cols], da[:, cols], half_gain[:], pb[:, cols], ALU.mult, ALU.mult)
         direct = wide("direct")
         nc.vector.scalar_tensor_tensor(direct[:], da[:], gain[:], w[:], ALU.mult, ALU.mult)
         linked = wide("linked")
-        nc.vector.tensor_tensor(linked[:], hs1[:].indirect(links[:]), pa_z[:], ALU.mult)
+        for cols, entries in zip(HALVES, LINK_HALVES):
+            nc.vector.tensor_tensor(linked[:, cols], hs1[:].indirect(links[:, entries]), pa_z[:, cols], ALU.mult)
 
         da_sq = column("da_sq")
         nc.scalar.activation(spare_a[:], da[:], ACT.Square, scale=rz[:], accum_out=da_sq[:])
@@ -153,10 +162,14 @@ def tile_attend_gplinkedproduct_kernel(tc, query, keys_words, keys_scales, gout,
         nc.scalar.activation(neg_da[:], da[:], ACT.Copy, scale=neg_rz[:])
 
         hdp = wide("hdp")
-        hdz = column("hdz")
-        nc.vector.scalar_tensor_tensor(hdp[:], linked[:], 1.0, direct[:], ALU.mult, ALU.add, accum_out=hdz[:])
+        hdz_parts = [column("hdz%d" % h) for h in range(2)]
+        for cols, part in zip(HALVES, hdz_parts):
+            nc.vector.scalar_tensor_tensor(hdp[:, cols], linked[:, cols], 1.0, direct[:, cols], ALU.mult, ALU.add, accum_out=part[:])
         r1 = wide("r1")
-        nc.vector.scalar_tensor_tensor(r1[:], c0[:], mean[:], hdp[:], ALU.subtract, ALU.mult)
+        for cols in HALVES:
+            nc.vector.scalar_tensor_tensor(r1[:, cols], c0[:, cols], mean[:], hdp[:, cols], ALU.subtract, ALU.mult)
+        hdz = column("hdz")
+        nc.scalar.activation(hdz[:], hdz_parts[0][:], ACT.Identity, bias=hdz_parts[1][:])
         sr = wide("sr", SCATTER_ADD_COLS)
         nc.vector.tensor_tensor(sr[:].indirect(links[:]), r1[:], y2[:], ALU.add)
         y3 = wide("y3")
@@ -174,5 +187,6 @@ def tile_attend_gplinkedproduct_kernel(tc, query, keys_words, keys_scales, gout,
             nc.tensor.transpose(rest[:, b * P : (b + 1) * P], turned_sb[:], ident[:])
 
         result = wide("result")
-        nc.vector.scalar_tensor_tensor(result[:], sr[:, :I], 0.5, rest[:], ALU.mult, ALU.add)
-        nc.sync.dma_start(out=out, in_=result[:])
+        for cols, queue in zip(HALVES, (nc.sync, nc.scalar)):
+            nc.vector.scalar_tensor_tensor(result[:, cols], sr[:, cols], 0.5, rest[:, cols], ALU.mult, ALU.add)
+            queue.dma_start(out=out[:, cols], in_=result[:, cols])

@@ -69,8 +69,6 @@ def tile_attend_gplinkedproduct_kernel(tc, query, keys_words, keys_scales, gout,
 
         warm = column("warm")
         nc.scalar.activation(warm[:], zero[:], ACT.Exp)
-        ident = sb.tile([P, P], F32, name="ident")
-        make_identity(nc, ident[:])
 
         def interleave(name, raw, offset):
             grouped = shared.tile([P, Q, PACK], BF16, name=name, align_bytes=64, offset=offset)
@@ -108,15 +106,19 @@ def tile_attend_gplinkedproduct_kernel(tc, query, keys_words, keys_scales, gout,
 
         pa = wide("pa")
         nc.scalar.activation(pb[:], a[:], ACT.Exp, scale=0.5)
-        nc.scalar.activation(pa[:], a[:], ACT.Exp)
+        for cols in HALVES:
+            nc.scalar.activation(pa[:, cols], a[:, cols], ACT.Exp)
         p = shared.tile([P, I], F32, name="p", align_bytes=64, offset=6144)
         for cols, entries in zip(HALVES, LINK_HALVES):
             nc.vector.tensor_tensor(p[:, cols], pb[:].indirect(links[:, entries]), pa[:, cols], ALU.mult)
         z_first = column("z_first")
         z = column("z")
         spare_a = wide("spare_a")
-        nc.scalar.activation(spare_a[:, HALVES[0]], p[:, HALVES[0]], ACT.Copy, scale=1.0 / HALF, accum_out=z_first[:])
+        spare_first = shared.tile([P, HALF], F32, name="spare_first", offset=12288)
+        nc.scalar.activation(spare_first[:], p[:, HALVES[0]], ACT.Copy, scale=1.0 / HALF, accum_out=z_first[:])
         nc.scalar.activation(spare_a[:, HALVES[1]], p[:, HALVES[1]], ACT.Identity, bias=z_first[:], accum_out=z[:])
+        ident = shared.tile([P, P], F32, name="ident", offset=12288)
+        make_identity(nc, ident[:])
         cp_sums = [column("cp_sum%d" % h) for h in range(2)]
         spare_v = wide("spare_v")
         for cols, cp_sum in zip(HALVES, cp_sums):

from contextlib import ExitStack

import concourse.mybir as mybir
from concourse.masks import make_identity

F32 = mybir.dt.float32
BF16 = mybir.dt.bfloat16
I32 = mybir.dt.int32
U32 = mybir.dt.uint32
U16 = mybir.dt.uint16
U8 = mybir.dt.uint8
FP8X4 = mybir.dt.float8_e4m3fn_x4
FP4X4 = mybir.dt.float4_e2m1fn_x4
ALU = mybir.AluOpType
ACT = mybir.ActivationFunctionType

P = 128
PACK = 4
D, T, I, Q = 512, 2048, 512, 128
GAIN = 512.0 * 2.0 * 512.0
HALF = I // 2
HALVES = (slice(0, HALF), slice(HALF, I))
LINK_HALVES = (slice(0, HALF // 16), slice(HALF // 16, I // 16))
SCATTER_COPY_COLS = 704
SCATTER_ADD_COLS = 1024
FLOPS = 2 * 2 * D * Q * I


def tile_attend_gplinkedproduct_kernel(tc, query, keys_words, keys_scales, gout, vals_words, vals_scales, base, offs2, offs, out):
    nc = tc.nc
    with ExitStack() as ctx:
        sb = ctx.enter_context(tc.tile_pool(name="sb", bufs=1))
        shared = ctx.enter_context(tc.tile_pool(name="shared", bufs=1))
        ps = ctx.enter_context(tc.psum_pool(name="ps", bufs=1))

        def wide(name, cols=I):
            return sb.tile([P, cols], F32, name=name, align_bytes=64)

        def column(name):
            return sb.tile([P, 1], F32, name=name)

        tokens = sb.tile([P, I // 16], U16, name="tokens")
        links = sb.tile([P, I // 16], U16, name="links")
        k_words = sb.tile([P, T], U16, name="k_words", align_bytes=64)
        v_words = sb.tile([P, T], U16, name="v_words", align_bytes=64)
        k_scales = shared.tile([P, T], U8, name="k_scales", align_bytes=64, offset=8192)
        v_scales = sb.tile([P, T], U8, name="v_scales", align_bytes=64)
        q_raw = shared.tile([P, PACK, Q], F32, name="q_raw", offset=6144)
        g_raw = shared.tile([P, PACK, Q], F32, name="g_raw", offset=2048)

        def load_scales(queue, tile, rows):
            for quad in range(4):
                queue.dma_start(out=tile[32 * quad : 32 * quad + 4, :].bitcast(I32), in_=rows[0, 4 * quad : 4 * quad + 4, :].bitcast(I32))

        pb = wide("pb")
        hs1 = wide("hs1")
        zero = column("zero")
        nc.gpsimd.memset(k_scales[:].bitcast(I32), 0)
        nc.gpsimd.memset(zero[:], 0.0)
        nc.vector.memset(v_scales[:].bitcast(I32), 0)
        nc.sync.dma_start(tokens[:], offs)
        nc.sync.dma_start(out=k_words[:].bitcast(I32), in_=keys_words[0].bitcast(I32))
        load_scales(nc.scalar, k_scales, keys_scales)
        nc.sync.dma_start(out=q_raw[:], in_=query.rearrange("(p j) w -> p j w", j=PACK))
        nc.gpsimd.dma_start(out=v_words[:].bitcast(I32), in_=vals_words[0].bitcast(I32))
        nc.gpsimd.dma_start(out=g_raw[:], in_=gout.rearrange("(p j) w -> p j w", j=PACK))
        load_scales(nc.sync, v_scales, vals_scales)
        nc.sync.dma_start(links[:], offs2)

        warm = column("warm")
        nc.scalar.activation(warm[:], zero[:], ACT.Exp)

        def interleave(name, raw, offset):
            grouped = shared.tile([P, Q, PACK], BF16, name=name, align_bytes=64, offset=offset)
            nc.scalar.copy(grouped[:], raw[:].rearrange("p j w -> p w j"))
            return grouped

        def quantize(name, grouped):
            codes = sb.tile([P, Q], U32, name=name + "_codes", align_bytes=64)
            scales = sb.tile([P, Q], U8, name=name + "_scales", align_bytes=64)
            nc.vector.quantize_mx(out=codes[:].bitcast(FP8X4), scales=scales[:], in_=grouped[:].rearrange("p w j -> p (w j)"))
            return codes, scales

        def gather(name, table, dtype, offset):
            picked = shared.tile([P, I], dtype, name=name, align_bytes=64, offset=offset)
            nc.vector.tensor_copy(picked[:], table[:].indirect(tokens[:]))
            return picked

        def product(name, codes, scales, words, word_scales):
            acc = ps.tile([P, I], F32, name=name)
            nc.tensor.matmul_mx(out=acc[:], lhsT=codes[:].bitcast(FP8X4), lhsT_scale=scales[:], rhs=words[:].bitcast(FP4X4), rhs_scale=word_scales[:], start=True, stop=True)
            return acc

        q_grouped = interleave("q_grouped", q_raw, 10240)
        ks = gather("ks", k_scales, U8, 4096)
        kw = gather("kw", k_words, U16, 5120)
        q_codes, q_scales = quantize("q", q_grouped)
        a = product("a", q_codes, q_scales, kw, ks)
        g_grouped = interleave("g_grouped", g_raw, 6144)
        base_sb = shared.tile([P, I], F32, name="base_sb", offset=2048)
        nc.sync.dma_start(out=base_sb[:], in_=base)
        vw = gather("vw", v_words, U16, 9728)
        vs = gather("vs", v_scales, U8, 0)
        g_codes, g_scales = quantize("g", g_grouped)
        c0 = product("c0", g_codes, g_scales, vw, vs)

        pa = wide("pa")
        nc.scalar.activation(pb[:], a[:], ACT.Exp, scale=0.5)
        for cols in HALVES:
            nc.scalar.activation(pa[:, cols], a[:, cols], ACT.Exp)
        p = shared.tile([P, I], F32, name="p", align_bytes=64, offset=6144)
        for cols, entries in zip(HALVES, LINK_HALVES):
            nc.vector.tensor_tensor(p[:, cols], pb[:].indirect(links[:, entries]), pa[:, cols], ALU.mult)
        z_first = column("z_first")
        z = column("z")
        spare_a = wide("spare_a")
        spare_first = shared.tile([P, HALF], F32, name="spare_first", offset=12288)
        nc.scalar.activation(spare_first[:], p[:, HALVES[0]], ACT.Copy, scale=1.0 / HALF, accum_out=z_first[:])
        nc.scalar.activation(spare_a[:, HALVES[1]], p[:, HALVES[1]], ACT.Identity, bias=z_first[:], accum_out=z[:])
        ident = shared.tile([P, P], F32, name="ident", offset=12288)
        make_identity(nc, ident[:])
        cp_sums = [column("cp_sum%d" % h) for h in range(2)]
        spare_v = wide("spare_v")
        for cols, cp_sum in zip(HALVES, cp_sums):
            nc.vector.scalar_tensor_tensor(spare_v[:, cols], c0[:, cols], 1.0, p[:, cols], ALU.mult, ALU.mult, accum_out=cp_sum[:])
        rz = column("rz")
        nc.vector.reciprocal(rz[:], z[:])
        mean = column("mean")
        nc.vector.tensor_scalar(mean[:], cp_sums[0][:], cp_sums[1][:], rz[:], ALU.add, ALU.mult)
        u = wide("u")
        nc.vector.scalar_tensor_tensor(u[:], c0[:], mean[:], p[:], ALU.subtract, ALU.mult)
        su = wide("su", SCATTER_COPY_COLS)
        nc.vector.tensor_copy(su[:].indirect(links[:]), u[:])

        w = wide("w")
        pa_z = wide("pa_z")
        nc.scalar.activation(w[:], p[:], ACT.Copy, scale=rz[:])
        nc.scalar.activation(pa_z[:], pa[:], ACT.Copy, scale=rz[:])
        half_gain = column("half_gain")
        gain = column("gain")
        neg_rz = column("neg_rz")
        nc.scalar.activation(half_gain[:], rz[:], ACT.Copy, scale=0.5 * GAIN)
        nc.scalar.activation(gain[:], rz[:], ACT.Copy, scale=GAIN)
        nc.scalar.activation(neg_rz[:], rz[:], ACT.Copy, scale=-1.0)
        neg_gain_w = wide("neg_gain_w")
        nc.scalar.activation(neg_gain_w[:], w[:], ACT.Copy, scale=-GAIN)

        da = wide("da")
        for cols in HALVES:
            nc.vector.scalar_tensor_tensor(da[:, cols], su[:, cols], 0.5, u[:, cols], ALU.mult, ALU.add)
        for cols in HALVES:
            nc.vector.scalar_tensor_tensor(hs1[:, cols], da[:, cols], half_gain[:], pb[:, cols], ALU.mult, ALU.mult)
        direct = wide("direct")
        nc.vector.scalar_tensor_tensor(direct[:], da[:], gain[:], w[:], ALU.mult, ALU.mult)
        linked = wide("linked")
        for cols, entries in zip(HALVES, LINK_HALVES):
            nc.vector.tensor_tensor(linked[:, cols], hs1[:].indirect(links[:, entries]), pa_z[:, cols], ALU.mult)

        da_sq = column("da_sq")
        nc.scalar.activation(spare_a[:], da[:], ACT.Square, scale=rz[:], accum_out=da_sq[:])
        y2 = wide("y2")
        nc.scalar.activation(y2[:], neg_gain_w[:], ACT.Copy, scale=da_sq[:])
        neg_da = wide("neg_da")
        nc.scalar.activation(neg_da[:], da[:], ACT.Copy, scale=neg_rz[:])

        hdp = wide("hdp")
        hdz_parts = [column("hdz%d" % h) for h in range(2)]
        for cols, part in zip(HALVES, hdz_parts):
            nc.vector.scalar_tensor_tensor(hdp[:, cols], linked[:, cols], 1.0, direct[:, cols], ALU.mult, ALU.add, accum_out=part[:])
        r1 = wide("r1")
        for cols in HALVES:
            nc.vector.scalar_tensor_tensor(r1[:, cols], c0[:, cols], mean[:], hdp[:, cols], ALU.subtract, ALU.mult)
        hdz = column("hdz")
        nc.scalar.activation(hdz[:], hdz_parts[0][:], ACT.Identity, bias=hdz_parts[1][:])
        sr = wide("sr", SCATTER_ADD_COLS)
        nc.vector.tensor_tensor(sr[:].indirect(links[:]), r1[:], y2[:], ALU.add)
        y3 = wide("y3")
        nc.scalar.activation(y3[:], neg_da[:], ACT.Copy, scale=hdz[:])

        terms = (y2, base_sb, r1, y3)
        turned = [ps.tile([P, P], F32, name="turned%d" % b) for b in range(I // P)]
        for n, term in enumerate(terms):
            for b in range(I // P):
                nc.tensor.matmul(turned[b][:], term[:, b * P : (b + 1) * P], ident[:], start=(n == 0), stop=(n == len(terms) - 1), is_transpose=True)
        rest = ps.tile([P, I], F32, name="rest")
        for b in range(I // P):
            turned_sb = sb.tile([P, P], F32, name="turned_sb%d" % b)
            nc.scalar.copy(turned_sb[:], turned[b][:])
            nc.tensor.transpose(rest[:, b * P : (b + 1) * P], turned_sb[:], ident[:])

        result = wide("result")
        for cols, queue in zip(HALVES, (nc.sync, nc.scalar)):
            nc.vector.scalar_tensor_tensor(result[:, cols], sr[:, cols], 0.5, rest[:, cols], ALU.mult, ALU.add)
            queue.dma_start(out=out[:, cols], in_=result[:, cols])
